import numpy as np
import ml_dtypes


def mxq(x, axis, fmt="e4m3"):
    dtype, down = {"e4m3": (ml_dtypes.float8_e4m3fn, 7), "e5m2": (ml_dtypes.float8_e5m2, 14)}[fmt]
    v = np.moveaxis(np.asarray(x, np.float32).astype(ml_dtypes.bfloat16).astype(np.float64), axis, -1)
    blocks = v.reshape(v.shape[:-1] + (-1, 32))
    amax = np.abs(blocks).max(-1, keepdims=True)
    byte = np.maximum(np.where(amax > 0, np.frexp(amax)[1] - 1 + 127, 0) - down, 1)
    scale = np.exp2(byte - 127.0)
    codes = (blocks / scale).astype(np.float32).astype(dtype).astype(np.float64)
    return np.moveaxis((codes * scale).reshape(v.shape), -1, axis)


WIDE = False


def mx_kscale(k):
    if not WIDE:
        return np.ones(k)
    levels = np.array([10, -10, 5, -5, 0])
    if k % 512:
        return np.exp2(np.random.permutation(np.resize(levels, k // 32))).repeat(32)
    a = np.empty((k // 512, 16))
    for p in range(k // 512):
        a[p, :8] = np.random.permutation(np.resize(levels, 8))
        for g in range(8):
            far = levels[np.abs(levels - a[p, g]) >= 10]
            a[p, g + 8] = far[np.random.randint(len(far))]
    return np.exp2(a.ravel()).repeat(32)


def f64(x):
    return np.asarray(x).astype(np.float64)


def striped(idx):
    return np.tile(idx.reshape(-1, 16).T, (8, 1)).astype(np.uint16)


def unstriped(offs):
    return offs[:16].T.reshape(-1).astype(np.int64)


def silu(v):
    return v / (1.0 + np.exp(-np.maximum(v, -700.0)))


K, T, E, C, H, N = 1536, 512, 4, 256, 512, 256


def by_expert(wq, xq):
    return np.concatenate([wq[e].T @ xq[:, e * C:(e + 1) * C] for e in range(E)], axis=1)


def setup_inputs():
    n = np.random.standard_normal
    s = mx_kscale(K)[:, None]
    u = mx_kscale(H)
    first = np.random.permutation(np.repeat(np.arange(E), T // E))
    second = (first + 1 + np.random.permutation(np.repeat(np.arange(E - 1), -(-T // (E - 1)))[:T])) % E
    while np.bincount(second, minlength=E).max() != T // E:
        load = np.bincount(second, minlength=E); hi, lo = int(load.argmax()), int(load.argmin())
        t = np.flatnonzero((second == hi) & (first != lo))[0]; second[t] = lo
    slot_token = np.empty(E * C, np.int64); pos = np.empty((2, T), np.int64); fill = np.zeros(E, np.int64)
    place = np.stack([np.random.permutation(C) for _ in range(E)])
    for r, deal in enumerate((first, second)):
        for t in np.random.permutation(T):
            e = deal[t]; j = e * C + place[e, fill[e]]; fill[e] += 1; slot_token[j] = t; pos[r, t] = j
    g = np.random.uniform(0.2, 0.8, T)
    return {
        "xT": (n((K, T)) * s).astype(np.float32),
        "w1": (n((E, K, H)) / np.sqrt(K) / s[None] * u[None, None, :]).astype(np.float32),
        "w2": (n((E, H, N)) / np.sqrt(H) / u[None, :, None]).astype(np.float32),
        "gate": np.stack([np.tile(g, (N, 1)), np.tile(1.0 - g, (N, 1))]).astype(np.float32),
        "offs": striped(slot_token),
        "pos1": striped(pos[0]),
        "pos2": striped(pos[1]),
    }


def reference(xT, w1, w2, gate, offs, pos1, pos2):
    idx = unstriped(offs)
    xq = mxq(f64(xT)[:, idx], 0, "e4m3")
    h = silu(by_expert(mxq(f64(w1), 1, "e4m3"), xq))
    y = by_expert(mxq(f64(w2), 1, "e4m3"), mxq(h, 0, "e4m3"))
    return f64(gate[0]) * y[:, unstriped(pos1)] + f64(gate[1]) * y[:, unstriped(pos2)]

@@ -1,0 +1,199 @@
+from contextlib import ExitStack
+
+import concourse.mybir as mybir
+
+K, T, E, C, H, N = 1536, 512, 4, 256, 512, 256
+P = 128
+PACK = 4
+K_PASS = P * PACK
+PASSES = K // K_PASS
+SLOTS = E * C
+HALF = 128
+N_BLOCKS = N // P
+
+FLOPS = 2 * SLOTS * (K * H + H * N)
+
+F32 = mybir.dt.float32
+BF16 = mybir.dt.bfloat16
+U32 = mybir.dt.uint32
+U16 = mybir.dt.uint16
+U8 = mybir.dt.uint8
+FP8X4 = mybir.dt.float8_e4m3fn_x4
+SILU = mybir.ActivationFunctionType.Silu
+MULT = mybir.AluOpType.mult
+
+GATHERS = ((0, 384), (384, 768), (768, 1024))
+
+X_VECTOR = 64
+W1_VECTOR = 48
+W2_VECTOR = 24
+
+
+def tile_routed_moe_kernel(tc, xT, w1, w2, gate, offs, pos1, pos2, out):
+    nc = tc.nc
+    with ExitStack() as ctx:
+        lists = ctx.enter_context(tc.tile_pool(name="lists", bufs=1))
+        raws = ctx.enter_context(tc.tile_pool(name="raws", bufs=1))
+        keep = ctx.enter_context(tc.tile_pool(name="keep", bufs=1))
+        work = ctx.enter_context(tc.tile_pool(name="work", bufs=1))
+        psum = ctx.enter_context(tc.psum_pool(name="psum", bufs=1))
+
+        offs_sb = lists.tile([P, SLOTS // 16], U16, name="offs_sb")
+        pos1_sb = lists.tile([P, T // 16], U16, name="pos1_sb")
+        pos2_sb = lists.tile([P, T // 16], U16, name="pos2_sb")
+
+        def split_copy(dst, src, share):
+            nc.vector.tensor_copy(out=dst[:, :share], in_=src[:, :share])
+            nc.scalar.copy(out=dst[:, share:], in_=src[:, share:])
+
+        warm = lists.tile([P, 1], F32, name="warm")
+        warmed = lists.tile([P, 1], F32, name="warmed")
+        nc.vector.memset(warm[:], 0.0)
+        nc.scalar.activation(out=warmed[:], in_=warm[:], func=SILU)
+
+        x_scales = keep.tile([P, T], U8, name="x_scales", align_bytes=64)
+        nc.gpsimd.memset(x_scales[:], 0)
+
+        def load_x(g, cuts):
+            t = raws.tile([P, PACK, T], F32, name="x_raw", bufs=PASSES)
+            src = xT[g * K_PASS : (g + 1) * K_PASS, :].rearrange("(p j) w -> p j w", j=PACK)
+            step = T // cuts
+            for c in range(cuts):
+                nc.sync.dma_start(out=t[:, :, c * step : (c + 1) * step], in_=src[:, :, c * step : (c + 1) * step])
+            return t
+
+        def load_w1(e, g, cuts):
+            t = raws.tile([P, PACK, H], F32, name="w1_raw", bufs=9)
+            src = w1[e, g * K_PASS : (g + 1) * K_PASS, :].rearrange("(p j) i -> p j i", j=PACK)
+            step = H // cuts
+            for c in range(cuts):
+                nc.sync.dma_start(out=t[:, :, c * step : (c + 1) * step], in_=src[:, :, c * step : (c + 1) * step])
+            return t
+
+        def load_w2(e):
+            t = raws.tile([P, PACK, N], F32, name="w2_raw", bufs=E)
+            nc.sync.dma_start(out=t[:], in_=w2[e, :, :].rearrange("(p j) n -> p j n", j=PACK))
+            return t
+
+        x_raw = [load_x(0, 2)]
+        nc.sync.dma_start(offs_sb[:], offs)
+        x_raw += [load_x(g, 1) for g in range(1, PASSES)]
+        nc.sync.dma_start(pos1_sb[:], pos1)
+        nc.sync.dma_start(pos2_sb[:], pos2)
+        w1_raw = {}
+        w2_raw = {}
+        for e in range(E):
+            for g in range(PASSES):
+                last = e == E - 1 and g == PASSES - 1
+                w1_raw[e, g] = load_w1(e, g, 2 if last else 1)
+            if e < 2:
+                w2_raw[e] = load_w2(e)
+        w2_raw[2] = load_w2(2)
+        w2_raw[3] = load_w2(3)
+        gate_sb = []
+        for b in range(N_BLOCKS):
+            t = raws.tile([P, 2, T], F32, name="gate_sb", bufs=N_BLOCKS)
+            nc.sync.dma_start(out=t[:], in_=gate[:, b * P : (b + 1) * P, :].rearrange("r p t -> p r t"))
+            gate_sb.append(t)
+
+        x_words = []
+        for g in range(PASSES):
+            grouped = work.tile([P, PACK * T], BF16, name="grouped", bufs=4, align_bytes=64)
+            dst = grouped[:].rearrange("p (c i j) -> p c j i", i=4, j=PACK)
+            src = x_raw[g][:].rearrange("p j (c i) -> p c j i", i=4)
+            cuts = 2 if g == 0 else 1
+            step = T // 4 // cuts
+            for c in range(cuts):
+                split_copy(dst[:, c * step : (c + 1) * step], src[:, c * step : (c + 1) * step], X_VECTOR // cuts)
+            words = keep.tile([P, T], U32, name="words", bufs=PASSES, align_bytes=64)
+            nc.vector.quantize_mx(out=words[:].bitcast(FP8X4), scales=x_scales[4 * g : P, :], in_=grouped[:])
+            x_words.append(words)
+
+        slot_words = keep.tile([P, PASSES, SLOTS], U32, name="slot_words", align_bytes=64)
+        slot_scales = keep.tile([P, SLOTS], U8, name="slot_scales", align_bytes=64)
+        y = [keep.tile([P, SLOTS], F32, name=f"y{b}") for b in range(N_BLOCKS)]
+
+        def gather(start, stop):
+            slots = slice(start, stop)
+            places = offs_sb[:, start // 16 : stop // 16]
+            for g in range(PASSES):
+                nc.vector.tensor_copy(out=slot_words[:, g, slots], in_=x_words[g][:].indirect(places))
+            nc.vector.tensor_copy(out=slot_scales[:, slots], in_=x_scales[:].indirect(places))
+
+        def quantize_w1(e, g, cuts):
+            grouped = work.tile([P, PACK * H], BF16, name="grouped", bufs=4, align_bytes=64)
+            dst = grouped[:].rearrange("p (t m j) -> p m j t", t=PACK, j=PACK)
+            src = w1_raw[e, g][:].rearrange("p j (m t) -> p m j t", t=PACK)
+            step = P // cuts
+            for c in range(cuts):
+                split_copy(dst[:, c * step : (c + 1) * step], src[:, c * step : (c + 1) * step], W1_VECTOR // cuts)
+            codes = keep.tile([P, H], U32, name="w1_codes", bufs=E * PASSES, align_bytes=64)
+            scales = keep.tile([P, H], U8, name="w1_scales", bufs=E * PASSES, align_bytes=64)
+            nc.vector.quantize_mx(out=codes[:].bitcast(FP8X4), scales=scales[:], in_=grouped[:])
+            return codes, scales
+
+        def quantize_w2(e):
+            grouped = work.tile([P, PACK * N], BF16, name="w2_grouped", bufs=2, align_bytes=64)
+            split_copy(
+                grouped[:].rearrange("p (c i j) -> p c j i", i=4, j=PACK),
+                w2_raw[e][:].rearrange("p j (c i) -> p c j i", i=4),
+                W2_VECTOR,
+            )
+            codes = keep.tile([P, N], U32, name="w2_codes", bufs=E, align_bytes=64)
+            scales = keep.tile([P, N], U8, name="w2_scales", bufs=E, align_bytes=64)
+            nc.vector.quantize_mx(out=codes[:].bitcast(FP8X4), scales=scales[:], in_=grouped[:])
+            return codes, scales
+
+        for e in range(E):
+            if e < len(GATHERS):
+                gather(*GATHERS[e])
+            sums = [psum.tile([P, PACK, HALF], F32, name="sums", bufs=4) for s in range(C // HALF)]
+            for g in range(PASSES):
+                codes, scales = quantize_w1(e, g, 2 if (e == E - 1 and g == PASSES - 1) else 1)
+                for s in range(C // HALF):
+                    slots = slice(e * C + s * HALF, e * C + (s + 1) * HALF)
+                    for t in range(PACK):
+                        cols = slice(t * P, (t + 1) * P)
+                        nc.tensor.matmul_mx(
+                            out=sums[s][:, t, :],
+                            lhsT=codes[:, cols].bitcast(FP8X4),
+                            lhsT_scale=scales[:, cols],
+                            rhs=slot_words[:, g, slots].bitcast(FP8X4),
+                            rhs_scale=slot_scales[4 * g : P, slots],
+                            start=(g == 0 and t == 0),
+                            stop=(g == PASSES - 1 and t == PACK - 1),
+                        )
+            w2_codes, w2_scales = quantize_w2(e)
+            y_sums = psum.tile([P, N_BLOCKS, C], F32, name="y_sums", bufs=4)
+            for s in range(C // HALF):
+                hidden = work.tile([P, PACK * HALF], BF16, name="hidden", bufs=4, align_bytes=64)
+                nc.scalar.activation(
+                    out=hidden[:].rearrange("p (n t) -> p n t", t=PACK),
+                    in_=sums[s][:].rearrange("p t n -> p n t"),
+                    func=SILU,
+                )
+                h_codes = work.tile([P, HALF], U32, name="h_codes", bufs=4, align_bytes=64)
+                h_scales = work.tile([P, HALF], U8, name="h_scales", bufs=4, align_bytes=64)
+                nc.vector.quantize_mx(out=h_codes[:].bitcast(FP8X4), scales=h_scales[:], in_=hidden[:])
+                for b in range(N_BLOCKS):
+                    cols = slice(b * P, (b + 1) * P)
+                    nc.tensor.matmul_mx(
+                        out=y_sums[:, b, s * HALF : (s + 1) * HALF],
+                        lhsT=w2_codes[:, cols].bitcast(FP8X4),
+                        lhsT_scale=w2_scales[:, cols],
+                        rhs=h_codes[:].bitcast(FP8X4),
+                        rhs_scale=h_scales[:],
+                        start=True,
+                        stop=True,
+                    )
+            for b in range(N_BLOCKS):
+                nc.scalar.copy(out=y[b][:, e * C : (e + 1) * C], in_=y_sums[:, b, :])
+
+        for b in range(N_BLOCKS):
+            first = work.tile([P, T], F32, name="first", bufs=2)
+            second = work.tile([P, T], F32, name="second", bufs=2)
+            total = work.tile([P, T], F32, name="total", bufs=2)
+            nc.vector.tensor_tensor(first[:], y[b][:].indirect(pos1_sb[:]), gate_sb[b][:, 0, :], MULT)
+            nc.vector.tensor_tensor(second[:], y[b][:].indirect(pos2_sb[:]), gate_sb[b][:, 1, :], MULT)
+            nc.vector.tensor_add(total[:], first[:], second[:])
+            nc.sync.dma_start(out=out[b * P : (b + 1) * P, :], in_=total[:])

@@ -22,11 +22,11 @@ FP8X4 = mybir.dt.float8_e4m3fn_x4
 SILU = mybir.ActivationFunctionType.Silu
 MULT = mybir.AluOpType.mult
 
-GATHERS = ((0, 384), (384, 768), (768, 1024))
+GATHERS = ((0, 256), (256, 640), (640, 1024))
 
-X_VECTOR = 64
-W1_VECTOR = 48
-W2_VECTOR = 24
+X_VECTOR = (64, 0, 128)
+W1_VECTOR = (0, 0, 0, 0, 128, 128, 0, 0, 128, 128, 128, 64)
+W2_VECTOR = (0, 0, 64, 64)
 
 
 def tile_routed_moe_kernel(tc, xT, w1, w2, gate, offs, pos1, pos2, out):
@@ -43,8 +43,10 @@ def tile_routed_moe_kernel(tc, xT, w1, w2, gate, offs, pos1, pos2, out):
         pos2_sb = lists.tile([P, T // 16], U16, name="pos2_sb")
 
         def split_copy(dst, src, share):
-            nc.vector.tensor_copy(out=dst[:, :share], in_=src[:, :share])
-            nc.scalar.copy(out=dst[:, share:], in_=src[:, share:])
+            if share > 0:
+                nc.vector.tensor_copy(out=dst[:, :share], in_=src[:, :share])
+            if share < dst.shape[1]:
+                nc.scalar.copy(out=dst[:, share:], in_=src[:, share:])
 
         warm = lists.tile([P, 1], F32, name="warm")
         warmed = lists.tile([P, 1], F32, name="warmed")
@@ -63,7 +65,7 @@ def tile_routed_moe_kernel(tc, xT, w1, w2, gate, offs, pos1, pos2, out):
             return t
 
         def load_w1(e, g, cuts):
-            t = raws.tile([P, PACK, H], F32, name="w1_raw", bufs=9)
+            t = raws.tile([P, PACK, H], F32, name="w_raw", bufs=10)
             src = w1[e, g * K_PASS : (g + 1) * K_PASS, :].rearrange("(p j) i -> p j i", j=PACK)
             step = H // cuts
             for c in range(cuts):
@@ -71,7 +73,7 @@ def tile_routed_moe_kernel(tc, xT, w1, w2, gate, offs, pos1, pos2, out):
             return t
 
         def load_w2(e):
-            t = raws.tile([P, PACK, N], F32, name="w2_raw", bufs=E)
+            t = raws.tile([P, PACK, N], F32, name="w_raw", bufs=10)
             nc.sync.dma_start(out=t[:], in_=w2[e, :, :].rearrange("(p j) n -> p j n", j=PACK))
             return t
 
@@ -86,13 +88,13 @@ def tile_routed_moe_kernel(tc, xT, w1, w2, gate, offs, pos1, pos2, out):
             for g in range(PASSES):
                 last = e == E - 1 and g == PASSES - 1
                 w1_raw[e, g] = load_w1(e, g, 2 if last else 1)
-            if e < 2:
+            if e == 0:
                 w2_raw[e] = load_w2(e)
-        w2_raw[2] = load_w2(2)
-        w2_raw[3] = load_w2(3)
+        for e in range(1, E):
+            w2_raw[e] = load_w2(e)
         gate_sb = []
         for b in range(N_BLOCKS):
-            t = raws.tile([P, 2, T], F32, name="gate_sb", bufs=N_BLOCKS)
+            t = raws.tile([P, 2, T], F32, name="w_raw", bufs=10)
             nc.sync.dma_start(out=t[:], in_=gate[:, b * P : (b + 1) * P, :].rearrange("r p t -> p r t"))
             gate_sb.append(t)
 
@@ -104,7 +106,7 @@ def tile_routed_moe_kernel(tc, xT, w1, w2, gate, offs, pos1, pos2, out):
             cuts = 2 if g == 0 else 1
             step = T // 4 // cuts
             for c in range(cuts):
-                split_copy(dst[:, c * step : (c + 1) * step], src[:, c * step : (c + 1) * step], X_VECTOR // cuts)
+                split_copy(dst[:, c * step : (c + 1) * step], src[:, c * step : (c + 1) * step], X_VECTOR[g] // cuts)
             words = keep.tile([P, T], U32, name="words", bufs=PASSES, align_bytes=64)
             nc.vector.quantize_mx(out=words[:].bitcast(FP8X4), scales=x_scales[4 * g : P, :], in_=grouped[:])
             x_words.append(words)
@@ -126,9 +128,9 @@ def tile_routed_moe_kernel(tc, xT, w1, w2, gate, offs, pos1, pos2, out):
             src = w1_raw[e, g][:].rearrange("p j (m t) -> p m j t", t=PACK)
             step = P // cuts
             for c in range(cuts):
-                split_copy(dst[:, c * step : (c + 1) * step], src[:, c * step : (c + 1) * step], W1_VECTOR // cuts)
-            codes = keep.tile([P, H], U32, name="w1_codes", bufs=E * PASSES, align_bytes=64)
-            scales = keep.tile([P, H], U8, name="w1_scales", bufs=E * PASSES, align_bytes=64)
+                split_copy(dst[:, c * step : (c + 1) * step], src[:, c * step : (c + 1) * step], W1_VECTOR[e * PASSES + g] // cuts)
+            codes = keep.tile([P, H], U32, name="w1_codes", bufs=8, align_bytes=64)
+            scales = keep.tile([P, H], U8, name="w1_scales", bufs=8, align_bytes=64)
             nc.vector.quantize_mx(out=codes[:].bitcast(FP8X4), scales=scales[:], in_=grouped[:])
             return codes, scales
 
@@ -137,16 +139,16 @@ def tile_routed_moe_kernel(tc, xT, w1, w2, gate, offs, pos1, pos2, out):
             split_copy(
                 grouped[:].rearrange("p (c i j) -> p c j i", i=4, j=PACK),
                 w2_raw[e][:].rearrange("p j (c i) -> p c j i", i=4),
-                W2_VECTOR,
+                W2_VECTOR[e],
             )
             codes = keep.tile([P, N], U32, name="w2_codes", bufs=E, align_bytes=64)
             scales = keep.tile([P, N], U8, name="w2_scales", bufs=E, align_bytes=64)
             nc.vector.quantize_mx(out=codes[:].bitcast(FP8X4), scales=scales[:], in_=grouped[:])
             return codes, scales
 
+        for start, stop in GATHERS:
+            gather(start, stop)
         for e in range(E):
-            if e < len(GATHERS):
-                gather(*GATHERS[e])
             sums = [psum.tile([P, PACK, HALF], F32, name="sums", bufs=4) for s in range(C // HALF)]
             for g in range(PASSES):
                 codes, scales = quantize_w1(e, g, 2 if (e == E - 1 and g == PASSES - 1) else 1)
@@ -165,35 +167,47 @@ def tile_routed_moe_kernel(tc, xT, w1, w2, gate, offs, pos1, pos2, out):
                         )
             w2_codes, w2_scales = quantize_w2(e)
             y_sums = psum.tile([P, N_BLOCKS, C], F32, name="y_sums", bufs=4)
+            pieces = 2 if e == E - 1 else 1
+            width = C // pieces
+            hidden = work.tile([P, PACK * C], BF16, name="hidden", bufs=2, align_bytes=64)
+            h_codes = work.tile([P, C], U32, name="h_codes", bufs=2, align_bytes=64)
+            h_scales = work.tile([P, C], U8, name="h_scales", bufs=2, align_bytes=64)
             for s in range(C // HALF):
-                hidden = work.tile([P, PACK * HALF], BF16, name="hidden", bufs=4, align_bytes=64)
                 nc.scalar.activation(
-                    out=hidden[:].rearrange("p (n t) -> p n t", t=PACK),
+                    out=hidden[:, s * PACK * HALF : (s + 1) * PACK * HALF].rearrange("p (n t) -> p n t", t=PACK),
                     in_=sums[s][:].rearrange("p t n -> p n t"),
                     func=SILU,
                 )
-                h_codes = work.tile([P, HALF], U32, name="h_codes", bufs=4, align_bytes=64)
-                h_scales = work.tile([P, HALF], U8, name="h_scales", bufs=4, align_bytes=64)
-                nc.vector.quantize_mx(out=h_codes[:].bitcast(FP8X4), scales=h_scales[:], in_=hidden[:])
+            for s in range(pieces):
+                slots = slice(s * width, (s + 1) * width)
+                nc.vector.quantize_mx(
+                    out=h_codes[:, slots].bitcast(FP8X4),
+                    scales=h_scales[:, slots],
+                    in_=hidden[:, PACK * s * width : PACK * (s + 1) * width],
+                )
                 for b in range(N_BLOCKS):
                     cols = slice(b * P, (b + 1) * P)
                     nc.tensor.matmul_mx(
-                        out=y_sums[:, b, s * HALF : (s + 1) * HALF],
+                        out=y_sums[:, b, slots],
                         lhsT=w2_codes[:, cols].bitcast(FP8X4),
                         lhsT_scale=w2_scales[:, cols],
-                        rhs=h_codes[:].bitcast(FP8X4),
-                        rhs_scale=h_scales[:],
+                        rhs=h_codes[:, slots].bitcast(FP8X4),
+                        rhs_scale=h_scales[:, slots],
                         start=True,
                         stop=True,
                     )
-            for b in range(N_BLOCKS):
-                nc.scalar.copy(out=y[b][:, e * C : (e + 1) * C], in_=y_sums[:, b, :])
+            if e < E - 1:
+                for b in range(N_BLOCKS):
+                    nc.scalar.copy(out=y[b][:, e * C : (e + 1) * C], in_=y_sums[:, b, :])
+            else:
+                for s in range(C // HALF):
+                    for b, copy in enumerate((nc.scalar.copy, nc.vector.tensor_copy)):
+                        copy(out=y[b][:, e * C + s * HALF : e * C + (s + 1) * HALF], in_=y_sums[:, b, s * HALF : (s + 1) * HALF])
 
         for b in range(N_BLOCKS):
-            first = work.tile([P, T], F32, name="first", bufs=2)
-            second = work.tile([P, T], F32, name="second", bufs=2)
-            total = work.tile([P, T], F32, name="total", bufs=2)
-            nc.vector.tensor_tensor(first[:], y[b][:].indirect(pos1_sb[:]), gate_sb[b][:, 0, :], MULT)
-            nc.vector.tensor_tensor(second[:], y[b][:].indirect(pos2_sb[:]), gate_sb[b][:, 1, :], MULT)
-            nc.vector.tensor_add(total[:], first[:], second[:])
-            nc.sync.dma_start(out=out[b * P : (b + 1) * P, :], in_=total[:])
+            parts = raws.tile([P, PACK, T], F32, name="x_raw", bufs=PASSES)
+            first, second, total = (parts[:, i, :] for i in range(3))
+            nc.vector.tensor_tensor(first, y[b][:].indirect(pos1_sb[:]), gate_sb[b][:, 0, :], MULT)
+            nc.vector.tensor_tensor(second, y[b][:].indirect(pos2_sb[:]), gate_sb[b][:, 1, :], MULT)
+            nc.vector.tensor_add(total, first, second)
+            nc.sync.dma_start(out=out[b * P : (b + 1) * P, :], in_=total)

@@ -22,10 +22,8 @@ FP8X4 = mybir.dt.float8_e4m3fn_x4
 SILU = mybir.ActivationFunctionType.Silu
 MULT = mybir.AluOpType.mult
 
-GATHERS = ((0, 256), (256, 640), (640, 1024))
-
-X_VECTOR = (64, 0, 128)
-W1_VECTOR = (0, 0, 0, 0, 128, 128, 0, 0, 128, 128, 128, 64)
+X_VECTOR = (64, 64, 64)
+W1_SHARES = ((0, 16), (32, 16), (56, 16), (0, 16), (112, 16), (32, 16), (56, 16), (0, 16), (128, 0), (32, 16), (128, 0), (72, 0))
 W2_VECTOR = (0, 0, 64, 64)
 
 
@@ -42,11 +40,16 @@ def tile_routed_moe_kernel(tc, xT, w1, w2, gate, offs, pos1, pos2, out):
         pos1_sb = lists.tile([P, T // 16], U16, name="pos1_sb")
         pos2_sb = lists.tile([P, T // 16], U16, name="pos2_sb")
 
-        def split_copy(dst, src, share):
+        def split_copy(dst, src, share, gpsimd=0):
+            rest = dst.shape[1] - gpsimd
             if share > 0:
                 nc.vector.tensor_copy(out=dst[:, :share], in_=src[:, :share])
-            if share < dst.shape[1]:
-                nc.scalar.copy(out=dst[:, share:], in_=src[:, share:])
+            if share < rest:
+                nc.scalar.copy(out=dst[:, share:rest], in_=src[:, share:rest])
+            if gpsimd > 0:
+                nc.gpsimd.tensor_scalar(
+                    out=dst[:, rest:], in0=src[:, rest:], scalar1=1.0, scalar2=0.0, op0=MULT, op1=mybir.AluOpType.add
+                )
 
         warm = lists.tile([P, 1], F32, name="warm")
         warmed = lists.tile([P, 1], F32, name="warmed")
@@ -111,16 +114,16 @@ def tile_routed_moe_kernel(tc, xT, w1, w2, gate, offs, pos1, pos2, out):
             nc.vector.quantize_mx(out=words[:].bitcast(FP8X4), scales=x_scales[4 * g : P, :], in_=grouped[:])
             x_words.append(words)
 
-        slot_words = keep.tile([P, PASSES, SLOTS], U32, name="slot_words", align_bytes=64)
-        slot_scales = keep.tile([P, SLOTS], U8, name="slot_scales", align_bytes=64)
         y = [keep.tile([P, SLOTS], F32, name=f"y{b}") for b in range(N_BLOCKS)]
 
-        def gather(start, stop):
-            slots = slice(start, stop)
-            places = offs_sb[:, start // 16 : stop // 16]
+        def gather(e):
+            slot_words = keep.tile([P, PASSES, C], U32, name="slot_words", bufs=2, align_bytes=64)
+            slot_scales = keep.tile([P, C], U8, name="slot_scales", bufs=2, align_bytes=64)
+            places = offs_sb[:, e * C // 16 : (e + 1) * C // 16]
             for g in range(PASSES):
-                nc.vector.tensor_copy(out=slot_words[:, g, slots], in_=x_words[g][:].indirect(places))
-            nc.vector.tensor_copy(out=slot_scales[:, slots], in_=x_scales[:].indirect(places))
+                nc.vector.tensor_copy(out=slot_words[:, g, :], in_=x_words[g][:].indirect(places))
+            nc.vector.tensor_copy(out=slot_scales[:], in_=x_scales[:].indirect(places))
+            return slot_words, slot_scales
 
         def quantize_w1(e, g, cuts):
             grouped = work.tile([P, PACK * H], BF16, name="grouped", bufs=4, align_bytes=64)
@@ -128,7 +131,11 @@ def tile_routed_moe_kernel(tc, xT, w1, w2, gate, offs, pos1, pos2, out):
             src = w1_raw[e, g][:].rearrange("p j (m t) -> p m j t", t=PACK)
             step = P // cuts
             for c in range(cuts):
-                split_copy(dst[:, c * step : (c + 1) * step], src[:, c * step : (c + 1) * step], W1_VECTOR[e * PASSES + g] // cuts)
+                split_copy(
+                    dst[:, c * step : (c + 1) * step],
+                    src[:, c * step : (c + 1) * step],
+                    *(share // cuts for share in W1_SHARES[e * PASSES + g]),
+                )
             codes = keep.tile([P, H], U32, name="w1_codes", bufs=8, align_bytes=64)
             scales = keep.tile([P, H], U8, name="w1_scales", bufs=8, align_bytes=64)
             nc.vector.quantize_mx(out=codes[:].bitcast(FP8X4), scales=scales[:], in_=grouped[:])
@@ -146,14 +153,13 @@ def tile_routed_moe_kernel(tc, xT, w1, w2, gate, offs, pos1, pos2, out):
             nc.vector.quantize_mx(out=codes[:].bitcast(FP8X4), scales=scales[:], in_=grouped[:])
             return codes, scales
 
-        for start, stop in GATHERS:
-            gather(start, stop)
         for e in range(E):
+            slot_words, slot_scales = gather(e)
             sums = [psum.tile([P, PACK, HALF], F32, name="sums", bufs=4) for s in range(C // HALF)]
             for g in range(PASSES):
                 codes, scales = quantize_w1(e, g, 2 if (e == E - 1 and g == PASSES - 1) else 1)
                 for s in range(C // HALF):
-                    slots = slice(e * C + s * HALF, e * C + (s + 1) * HALF)
+                    slots = slice(s * HALF, (s + 1) * HALF)
                     for t in range(PACK):
                         cols = slice(t * P, (t + 1) * P)
                         nc.tensor.matmul_mx(

@@ -80,7 +80,7 @@ def tile_routed_moe_kernel(tc, xT, w1, w2, gate, offs, pos1, pos2, out):
             nc.sync.dma_start(out=t[:], in_=w2[e, :, :].rearrange("(p j) n -> p j n", j=PACK))
             return t
 
-        x_raw = [load_x(0, 2)]
+        x_raw = [load_x(0, 1)]
         nc.sync.dma_start(offs_sb[:], offs)
         x_raw += [load_x(g, 1) for g in range(1, PASSES)]
         nc.sync.dma_start(pos1_sb[:], pos1)
@@ -90,7 +90,7 @@ def tile_routed_moe_kernel(tc, xT, w1, w2, gate, offs, pos1, pos2, out):
         for e in range(E):
             for g in range(PASSES):
                 last = e == E - 1 and g == PASSES - 1
-                w1_raw[e, g] = load_w1(e, g, 2 if last else 1)
+                w1_raw[e, g] = load_w1(e, g, 1)
             if e == 0:
                 w2_raw[e] = load_w2(e)
         for e in range(1, E):
@@ -106,7 +106,7 @@ def tile_routed_moe_kernel(tc, xT, w1, w2, gate, offs, pos1, pos2, out):
             grouped = work.tile([P, PACK * T], BF16, name="grouped", bufs=4, align_bytes=64)
             dst = grouped[:].rearrange("p (c i j) -> p c j i", i=4, j=PACK)
             src = x_raw[g][:].rearrange("p j (c i) -> p c j i", i=4)
-            cuts = 2 if g == 0 else 1
+            cuts = 1
             step = T // 4 // cuts
             for c in range(cuts):
                 split_copy(dst[:, c * step : (c + 1) * step], src[:, c * step : (c + 1) * step], X_VECTOR[g] // cuts)
@@ -157,7 +157,7 @@ def tile_routed_moe_kernel(tc, xT, w1, w2, gate, offs, pos1, pos2, out):
             slot_words, slot_scales = gather(e)
             sums = [psum.tile([P, PACK, HALF], F32, name="sums", bufs=4) for s in range(C // HALF)]
             for g in range(PASSES):
-                codes, scales = quantize_w1(e, g, 2 if (e == E - 1 and g == PASSES - 1) else 1)
+                codes, scales = quantize_w1(e, g, 1)
                 for s in range(C // HALF):
                     slots = slice(s * HALF, (s + 1) * HALF)
                     for t in range(PACK):
@@ -215,5 +215,6 @@ def tile_routed_moe_kernel(tc, xT, w1, w2, gate, offs, pos1, pos2, out):
             first, second, total = (parts[:, i, :] for i in range(3))
             nc.vector.tensor_tensor(first, y[b][:].indirect(pos1_sb[:]), gate_sb[b][:, 0, :], MULT)
             nc.vector.tensor_tensor(second, y[b][:].indirect(pos2_sb[:]), gate_sb[b][:, 1, :], MULT)
-            nc.vector.tensor_add(total, first, second)
-            nc.sync.dma_start(out=out[b * P : (b + 1) * P, :], in_=total)
+            for cols in (slice(0, T // 2), slice(T // 2, T)):
+                nc.vector.tensor_add(total[:, cols], first[:, cols], second[:, cols])
+                nc.sync.dma_start(out=out[b * P : (b + 1) * P, cols], in_=total[:, cols])

from contextlib import ExitStack

import concourse.mybir as mybir

K, T, E, C, H, N = 1536, 512, 4, 256, 512, 256
P = 128
PACK = 4
K_PASS = P * PACK
PASSES = K // K_PASS
SLOTS = E * C
HALF = 128
N_BLOCKS = N // P

FLOPS = 2 * SLOTS * (K * H + H * N)

F32 = mybir.dt.float32
BF16 = mybir.dt.bfloat16
U32 = mybir.dt.uint32
U16 = mybir.dt.uint16
U8 = mybir.dt.uint8
FP8X4 = mybir.dt.float8_e4m3fn_x4
SILU = mybir.ActivationFunctionType.Silu
MULT = mybir.AluOpType.mult

X_VECTOR = (64, 64, 64)
W1_SHARES = ((0, 16), (32, 16), (56, 16), (0, 16), (112, 16), (32, 16), (56, 16), (0, 16), (128, 0), (32, 16), (128, 0), (72, 0))
W2_VECTOR = (0, 0, 64, 64)


def tile_routed_moe_kernel(tc, xT, w1, w2, gate, offs, pos1, pos2, out):
    nc = tc.nc
    with ExitStack() as ctx:
        lists = ctx.enter_context(tc.tile_pool(name="lists", bufs=1))
        raws = ctx.enter_context(tc.tile_pool(name="raws", bufs=1))
        keep = ctx.enter_context(tc.tile_pool(name="keep", bufs=1))
        work = ctx.enter_context(tc.tile_pool(name="work", bufs=1))
        psum = ctx.enter_context(tc.psum_pool(name="psum", bufs=1))

        offs_sb = lists.tile([P, SLOTS // 16], U16, name="offs_sb")
        pos1_sb = lists.tile([P, T // 16], U16, name="pos1_sb")
        pos2_sb = lists.tile([P, T // 16], U16, name="pos2_sb")

        def split_copy(dst, src, share, gpsimd=0):
            rest = dst.shape[1] - gpsimd
            if share > 0:
                nc.vector.tensor_copy(out=dst[:, :share], in_=src[:, :share])
            if share < rest:
                nc.scalar.copy(out=dst[:, share:rest], in_=src[:, share:rest])
            if gpsimd > 0:
                nc.gpsimd.tensor_scalar(
                    out=dst[:, rest:], in0=src[:, rest:], scalar1=1.0, scalar2=0.0, op0=MULT, op1=mybir.AluOpType.add
                )

        warm = lists.tile([P, 1], F32, name="warm")
        warmed = lists.tile([P, 1], F32, name="warmed")
        nc.vector.memset(warm[:], 0.0)
        nc.scalar.activation(out=warmed[:], in_=warm[:], func=SILU)

        x_scales = keep.tile([P, T], U8, name="x_scales", align_bytes=64)
        nc.gpsimd.memset(x_scales[:], 0)

        def load_x(g, cuts):
            t = raws.tile([P, PACK, T], F32, name="x_raw", bufs=PASSES)
            src = xT[g * K_PASS : (g + 1) * K_PASS, :].rearrange("(p j) w -> p j w", j=PACK)
            step = T // cuts
            for c in range(cuts):
                nc.sync.dma_start(out=t[:, :, c * step : (c + 1) * step], in_=src[:, :, c * step : (c + 1) * step])
            return t

        def load_w1(e, g, cuts):
            t = raws.tile([P, PACK, H], F32, name="w_raw", bufs=10)
            src = w1[e, g * K_PASS : (g + 1) * K_PASS, :].rearrange("(p j) i -> p j i", j=PACK)
            step = H // cuts
            for c in range(cuts):
                nc.sync.dma_start(out=t[:, :, c * step : (c + 1) * step], in_=src[:, :, c * step : (c + 1) * step])
            return t

        def load_w2(e):
            t = raws.tile([P, PACK, N], F32, name="w_raw", bufs=10)
            nc.sync.dma_start(out=t[:], in_=w2[e, :, :].rearrange("(p j) n -> p j n", j=PACK))
            return t

        x_raw = [load_x(0, 1)]
        nc.sync.dma_start(offs_sb[:], offs)
        x_raw += [load_x(g, 1) for g in range(1, PASSES)]
        nc.sync.dma_start(pos1_sb[:], pos1)
        nc.sync.dma_start(pos2_sb[:], pos2)
        w1_raw = {}
        w2_raw = {}
        for e in range(E):
            for g in range(PASSES):
                last = e == E - 1 and g == PASSES - 1
                w1_raw[e, g] = load_w1(e, g, 1)
            if e == 0:
                w2_raw[e] = load_w2(e)
        for e in range(1, E):
            w2_raw[e] = load_w2(e)
        gate_sb = []
        for b in range(N_BLOCKS):
            t = raws.tile([P, 2, T], F32, name="w_raw", bufs=10)
            nc.sync.dma_start(out=t[:], in_=gate[:, b * P : (b + 1) * P, :].rearrange("r p t -> p r t"))
            gate_sb.append(t)

        x_words = []
        for g in range(PASSES):
            grouped = work.tile([P, PACK * T], BF16, name="grouped", bufs=4, align_bytes=64)
            dst = grouped[:].rearrange("p (c i j) -> p c j i", i=4, j=PACK)
            src = x_raw[g][:].rearrange("p j (c i) -> p c j i", i=4)
            cuts = 1
            step = T // 4 // cuts
            for c in range(cuts):
                split_copy(dst[:, c * step : (c + 1) * step], src[:, c * step : (c + 1) * step], X_VECTOR[g] // cuts)
            words = keep.tile([P, T], U32, name="words", bufs=PASSES, align_bytes=64)
            nc.vector.quantize_mx(out=words[:].bitcast(FP8X4), scales=x_scales[4 * g : P, :], in_=grouped[:])
            x_words.append(words)

        y = [keep.tile([P, SLOTS], F32, name=f"y{b}") for b in range(N_BLOCKS)]

        def gather(e):
            slot_words = keep.tile([P, PASSES, C], U32, name="slot_words", bufs=2, align_bytes=64)
            slot_scales = keep.tile([P, C], U8, name="slot_scales", bufs=2, align_bytes=64)
            places = offs_sb[:, e * C // 16 : (e + 1) * C // 16]
            for g in range(PASSES):
                nc.vector.tensor_copy(out=slot_words[:, g, :], in_=x_words[g][:].indirect(places))
            nc.vector.tensor_copy(out=slot_scales[:], in_=x_scales[:].indirect(places))
            return slot_words, slot_scales

        def quantize_w1(e, g, cuts):
            grouped = work.tile([P, PACK * H], BF16, name="grouped", bufs=4, align_bytes=64)
            dst = grouped[:].rearrange("p (t m j) -> p m j t", t=PACK, j=PACK)
            src = w1_raw[e, g][:].rearrange("p j (m t) -> p m j t", t=PACK)
            step = P // cuts
            for c in range(cuts):
                split_copy(
                    dst[:, c * step : (c + 1) * step],
                    src[:, c * step : (c + 1) * step],
                    *(share // cuts for share in W1_SHARES[e * PASSES + g]),
                )
            codes = keep.tile([P, H], U32, name="w1_codes", bufs=8, align_bytes=64)
            scales = keep.tile([P, H], U8, name="w1_scales", bufs=8, align_bytes=64)
            nc.vector.quantize_mx(out=codes[:].bitcast(FP8X4), scales=scales[:], in_=grouped[:])
            return codes, scales

        def quantize_w2(e):
            grouped = work.tile([P, PACK * N], BF16, name="w2_grouped", bufs=2, align_bytes=64)
            split_copy(
                grouped[:].rearrange("p (c i j) -> p c j i", i=4, j=PACK),
                w2_raw[e][:].rearrange("p j (c i) -> p c j i", i=4),
                W2_VECTOR[e],
            )
            codes = keep.tile([P, N], U32, name="w2_codes", bufs=E, align_bytes=64)
            scales = keep.tile([P, N], U8, name="w2_scales", bufs=E, align_bytes=64)
            nc.vector.quantize_mx(out=codes[:].bitcast(FP8X4), scales=scales[:], in_=grouped[:])
            return codes, scales

        for e in range(E):
            slot_words, slot_scales = gather(e)
            sums = [psum.tile([P, PACK, HALF], F32, name="sums", bufs=4) for s in range(C // HALF)]
            for g in range(PASSES):
                codes, scales = quantize_w1(e, g, 1)
                for s in range(C // HALF):
                    slots = slice(s * HALF, (s + 1) * HALF)
                    for t in range(PACK):
                        cols = slice(t * P, (t + 1) * P)
                        nc.tensor.matmul_mx(
                            out=sums[s][:, t, :],
                            lhsT=codes[:, cols].bitcast(FP8X4),
                            lhsT_scale=scales[:, cols],
                            rhs=slot_words[:, g, slots].bitcast(FP8X4),
                            rhs_scale=slot_scales[4 * g : P, slots],
                            start=(g == 0 and t == 0),
                            stop=(g == PASSES - 1 and t == PACK - 1),
                        )
            w2_codes, w2_scales = quantize_w2(e)
            y_sums = psum.tile([P, N_BLOCKS, C], F32, name="y_sums", bufs=4)
            pieces = 2 if e == E - 1 else 1
            width = C // pieces
            hidden = work.tile([P, PACK * C], BF16, name="hidden", bufs=2, align_bytes=64)
            h_codes = work.tile([P, C], U32, name="h_codes", bufs=2, align_bytes=64)
            h_scales = work.tile([P, C], U8, name="h_scales", bufs=2, align_bytes=64)
            for s in range(C // HALF):
                nc.scalar.activation(
                    out=hidden[:, s * PACK * HALF : (s + 1) * PACK * HALF].rearrange("p (n t) -> p n t", t=PACK),
                    in_=sums[s][:].rearrange("p t n -> p n t"),
                    func=SILU,
                )
            for s in range(pieces):
                slots = slice(s * width, (s + 1) * width)
                nc.vector.quantize_mx(
                    out=h_codes[:, slots].bitcast(FP8X4),
                    scales=h_scales[:, slots],
                    in_=hidden[:, PACK * s * width : PACK * (s + 1) * width],
                )
                for b in range(N_BLOCKS):
                    cols = slice(b * P, (b + 1) * P)
                    nc.tensor.matmul_mx(
                        out=y_sums[:, b, slots],
                        lhsT=w2_codes[:, cols].bitcast(FP8X4),
                        lhsT_scale=w2_scales[:, cols],
                        rhs=h_codes[:, slots].bitcast(FP8X4),
                        rhs_scale=h_scales[:, slots],
                        start=True,
                        stop=True,
                    )
            if e < E - 1:
                for b in range(N_BLOCKS):
                    nc.scalar.copy(out=y[b][:, e * C : (e + 1) * C], in_=y_sums[:, b, :])
            else:
                for s in range(C // HALF):
                    for b, copy in enumerate((nc.scalar.copy, nc.vector.tensor_copy)):
                        copy(out=y[b][:, e * C + s * HALF : e * C + (s + 1) * HALF], in_=y_sums[:, b, s * HALF : (s + 1) * HALF])

        for b in range(N_BLOCKS):
            parts = raws.tile([P, PACK, T], F32, name="x_raw", bufs=PASSES)
            first, second, total = (parts[:, i, :] for i in range(3))
            nc.vector.tensor_tensor(first, y[b][:].indirect(pos1_sb[:]), gate_sb[b][:, 0, :], MULT)
            nc.vector.tensor_tensor(second, y[b][:].indirect(pos2_sb[:]), gate_sb[b][:, 1, :], MULT)
            for cols in (slice(0, T // 2), slice(T // 2, T)):
                nc.vector.tensor_add(total[:, cols], first[:, cols], second[:, cols])
                nc.sync.dma_start(out=out[b * P : (b + 1) * P, cols], in_=total[:, cols])
